import numpy as np
import ml_dtypes


def mxq(x, axis, fmt="e4m3"):
    dtype, down = {"e4m3": (ml_dtypes.float8_e4m3fn, 7), "e5m2": (ml_dtypes.float8_e5m2, 14)}[fmt]
    v = np.moveaxis(np.asarray(x, np.float32).astype(ml_dtypes.bfloat16).astype(np.float64), axis, -1)
    blocks = v.reshape(v.shape[:-1] + (-1, 32))
    amax = np.abs(blocks).max(-1, keepdims=True)
    byte = np.maximum(np.where(amax > 0, np.frexp(amax)[1] - 1 + 127, 0) - down, 1)
    scale = np.exp2(byte - 127.0)
    codes = (blocks / scale).astype(np.float32).astype(dtype).astype(np.float64)
    return np.moveaxis((codes * scale).reshape(v.shape), -1, axis)


WIDE = False


def mx_kscale(k):
    if not WIDE:
        return np.ones(k)
    levels = np.array([10, -10, 5, -5, 0])
    if k % 512:
        return np.exp2(np.random.permutation(np.resize(levels, k // 32))).repeat(32)
    a = np.empty((k // 512, 16))
    for p in range(k // 512):
        a[p, :8] = np.random.permutation(np.resize(levels, 8))
        for g in range(8):
            far = levels[np.abs(levels - a[p, g]) >= 10]
            a[p, g + 8] = far[np.random.randint(len(far))]
    return np.exp2(a.ravel()).repeat(32)


def f64(x):
    return np.asarray(x).astype(np.float64)


def striped8(idx):
    return np.asarray(idx).reshape(8, -1, 16).transpose(0, 2, 1).reshape(128, -1).astype(np.uint16)


def unstriped8(offs):
    return offs.reshape(8, 16, -1).transpose(0, 2, 1).reshape(8, -1).astype(np.int64)


def pick8(x, idx, run):
    r = np.arange(len(x))
    return x[r[:, None], idx[r % (8 * run) // run]]


E2M1 = np.array([0.0, 0.5, 1.0, 1.5, 2.0, 3.0, 4.0, 6.0, -0.0, -0.5, -1.0, -1.5, -2.0, -3.0, -4.0, -6.0])


def pack_weight(w, fmt):
    k, n = w.shape
    w = f64(np.asarray(w, np.float32).astype(ml_dtypes.bfloat16)).reshape(k // 32, 32, n)
    amax = np.abs(w).max(1)
    if fmt == "e4m3":
        byte = np.frexp(amax)[1] - 1 + 127 - 7
    else:
        mant, ex = np.frexp(amax / 6.0)
        byte = np.where(mant > 0.5, ex, ex - 1) + 127
    byte = np.clip(np.where(amax > 0, byte, 1), 1, 254)
    scaled = (w * np.exp2(127.0 - byte)[:, None, :]).reshape(k, n).astype(np.float32)
    by_word = np.ascontiguousarray(scaled.reshape(k // 512, 128, 4, n).transpose(0, 1, 3, 2))
    if fmt == "e4m3":
        words = by_word.astype(ml_dtypes.float8_e4m3fn).view(np.uint8)
    else:
        c = by_word.astype(ml_dtypes.float4_e2m1fn).view(np.uint8) & 0xF
        words = (c[..., 0::2] | (c[..., 1::2] << 4)).reshape(k // 512, 128, 2 * n)
    return np.ascontiguousarray(words), np.ascontiguousarray(byte.astype(np.uint8).reshape(k // 512, 16, n))


def unpack_weight(words, scales, fmt):
    g, _, n = scales.shape
    words = np.ascontiguousarray(words).reshape(g, 128, n, -1)
    if fmt == "e4m3":
        vals = words.view(ml_dtypes.float8_e4m3fn).astype(np.float64)
    else:
        nib = np.empty((g, 128, n, 4), np.uint8)
        nib[..., 0::2] = words & 0xF
        nib[..., 1::2] = words >> 4
        vals = E2M1[nib]
    vals = vals * np.repeat(np.exp2(scales.astype(np.float64) - 127.0), 8, axis=1)[..., None]
    return vals.transpose(0, 1, 3, 2).reshape(g * 512, n)


def sgn(shape):
    return np.random.uniform(0.5, 2.0, shape) * np.where(np.random.standard_normal(shape) < 0, -1.0, 1.0)


D, K, T, U, X, I, Q = 512, 512, 1024, 1024, 1024, 512, 128


def setup_inputs():
    n = np.random.standard_normal
    idx = np.stack([np.random.permutation(T)[:I] for _ in range(8)])
    idx2 = np.stack([np.random.permutation(U)[:I] for _ in range(8)])
    idx3 = np.stack([np.random.permutation(U)[:I] for _ in range(8)])
    idx4 = np.stack([np.random.permutation(X)[:I] for _ in range(8)])
    idx5 = np.stack([np.random.permutation(X)[:I] for _ in range(8)])
    fd = mx_kscale(D)
    fk = mx_kscale(K)
    wqp = pack_weight(n((D, K)) * 1.0 / np.sqrt(D) * fd[:, None] * fk, "e4m3")
    cachep = pack_weight(n((K, T)) * 1.0 / np.sqrt(K) / fk[:, None], "e2m1")
    draftp = pack_weight(n((K, U)) * 1.0 / np.sqrt(K) / fk[:, None], "e4m3")
    archp = pack_weight(n((D, X)) * 1.0 / np.sqrt(D) * fd[:, None], "e2m1")
    return {
        "states": (n((D, Q)) * 0.95 / fd[:, None]).astype(np.float32),
        "wq_words": wqp[0],
        "wq_scales": wqp[1],
        "cache_words": cachep[0],
        "cache_scales": cachep[1],
        "draft_words": draftp[0],
        "draft_scales": draftp[1],
        "arch_words": archp[0],
        "arch_scales": archp[1],
        "sa": (sgn((Q, 1))).astype(np.float32),
        "sb": (sgn((Q, 1))).astype(np.float32),
        "offs": striped8(idx),
        "offs2": striped8(idx2),
        "offs3": striped8(idx3),
        "offs4": striped8(idx4),
        "offs5": striped8(idx5),
    }


def reference(states, wq_words, wq_scales, cache_words, cache_scales, draft_words, draft_scales, arch_words, arch_scales, sa, sb, offs, offs2, offs3, offs4, offs5):
    idx = unstriped8(offs)
    idx2 = unstriped8(offs2)
    idx3 = unstriped8(offs3)
    idx4 = unstriped8(offs4)
    idx5 = unstriped8(offs5)
    wqu = unpack_weight(wq_words, wq_scales, "e4m3")
    cacheu = unpack_weight(cache_words, cache_scales, "e2m1")
    draftu = unpack_weight(draft_words, draft_scales, "e4m3")
    archu = unpack_weight(arch_words, arch_scales, "e2m1")
    statesq = mxq(f64(states), 0, "e4m3")
    qv = wqu.T @ statesq
    qvq = mxq(qv, 0, "e4m3")
    a = qvq.T @ cacheu
    b = qvq.T @ draftu
    c0 = statesq.T @ archu
    w = pick8(a, idx, 16) * f64(sa)
    f1 = np.zeros((Q, U))
    f1[np.arange(Q)[:, None], idx2[np.arange(Q) % 128 // 16]] = w
    bb = b - f1
    v = pick8(bb, idx3, 16) * f64(sb)
    f2 = np.zeros((Q, X))
    f2[np.arange(Q)[:, None], idx4[np.arange(Q) % 128 // 16]] = v
    cc = np.maximum(c0, f2)
    y = pick8(cc, idx5, 16)
    return y

@@ -1,0 +1,149 @@
+from contextlib import ExitStack
+
+import concourse.mybir as mybir
+
+D, K, T, U, X, I, Q = 512, 512, 1024, 1024, 1024, 512, 128
+FLOPS = 2 * Q * (D * K + K * T + K * U + D * X)
+
+F32 = mybir.dt.float32
+BF16 = mybir.dt.bfloat16
+I32 = mybir.dt.int32
+U32 = mybir.dt.uint32
+U16 = mybir.dt.uint16
+U8 = mybir.dt.uint8
+FP8X4 = mybir.dt.float8_e4m3fn_x4
+FP4X4 = mybir.dt.float4_e2m1fn_x4
+COPY = mybir.ActivationFunctionType.Copy
+ALU = mybir.AluOpType
+
+P = 128
+PACK = 4
+BANK = 512
+A_PIECE = 256
+
+
+def tile_attend_scaledhops_sidethree_kernel(tc, states, wq_words, wq_scales, cache_words, cache_scales, draft_words,
+                                             draft_scales, arch_words, arch_scales, sa, sb, offs, offs2, offs3,
+                                             offs4, offs5, out):
+    nc = tc.nc
+    with ExitStack() as ctx:
+        pool = ctx.enter_context(tc.tile_pool(name="held", bufs=1))
+        psum = ctx.enter_context(tc.psum_pool(name="psum", bufs=1))
+
+        def zeroed(name, width, dtype):
+            t = pool.tile([P, width], dtype, name=name, align_bytes=64)
+            nc.vector.memset(t[:].bitcast(I32), 0)
+            return t
+
+        def load_plane(plane, scales):
+            for g in range(4):
+                nc.sync.dma_start(plane[32 * g : 32 * g + 4, :].bitcast(I32), scales[0, 4 * g : 4 * g + 4, :].bitcast(I32))
+
+        def load_bytes(name, src):
+            t = pool.tile([P, src.shape[1]], U8, name=name, align_bytes=64)
+            nc.sync.dma_start(t[:].bitcast(I32), src.bitcast(I32))
+            return t
+
+        def load_as_is(name, src, dtype):
+            t = pool.tile(list(src.shape), dtype, name=name)
+            nc.sync.dma_start(t[:], src)
+            return t
+
+        wq_plane_raw = zeroed("wq_plane_raw", K, U8)
+        cache_plane = zeroed("cache_plane", T, U8)
+        draft_plane = zeroed("draft_plane", U, U8)
+        arch_plane = zeroed("arch_plane", X, U8)
+        f1 = pool.tile([P, U], F32, name="f1")
+        nc.vector.memset(f1[:], 0.0)
+        f2 = pool.tile([P, X], F32, name="f2")
+        nc.vector.memset(f2[:], 0.0)
+
+        states_raw = pool.tile([P, PACK, Q], F32, name="states_raw")
+        nc.sync.dma_start(states_raw[:], states.rearrange("(p j) q -> p j q", j=PACK))
+        load_plane(wq_plane_raw, wq_scales)
+        wq_raw = load_bytes("wq_raw", wq_words[0].rearrange("p n t -> p (n t)"))
+        cache_sb = load_bytes("cache_sb", cache_words[0])
+        load_plane(cache_plane, cache_scales)
+        list1 = load_as_is("list1", offs, U16)
+        sa_sb = load_as_is("sa_sb", sa, F32)
+        list2 = load_as_is("list2", offs2, U16)
+        draft_sb = load_bytes("draft_sb", draft_words[0].rearrange("p n t -> p (n t)"))
+        load_plane(draft_plane, draft_scales)
+        list3 = load_as_is("list3", offs3, U16)
+        sb_sb = load_as_is("sb_sb", sb, F32)
+        list4 = load_as_is("list4", offs4, U16)
+        arch_sb = load_bytes("arch_sb", arch_words[0])
+        load_plane(arch_plane, arch_scales)
+        list5 = load_as_is("list5", offs5, U16)
+
+        wq_plane = pool.tile([P, PACK, P], U8, name="wq_plane", align_bytes=64)
+        nc.vector.tensor_copy(wq_plane[:].rearrange("p t m -> p m t"), wq_plane_raw[:].rearrange("p (m t) -> p m t", t=PACK))
+
+        states_bf = pool.tile([P, Q, PACK], BF16, name="states_bf", align_bytes=64)
+        nc.vector.tensor_copy(states_bf[:].rearrange("p (c i) t -> p c t i", i=4),
+                              states_raw[:].rearrange("p t (c i) -> p c t i", i=4))
+        states_codes = pool.tile([P, Q], U32, name="states_codes", align_bytes=64)
+        states_plane = pool.tile([P, Q], U8, name="states_plane", align_bytes=64)
+        nc.vector.quantize_mx(out=states_codes[:].bitcast(FP8X4), scales=states_plane[:],
+                              in_=states_bf[:].rearrange("p q t -> p (q t)"))
+
+        wq_dealt = pool.tile([P, PACK, P], U32, name="wq_dealt", align_bytes=64)
+        nc.scalar.copy(wq_dealt[:].rearrange("p t m -> p m t"),
+                       wq_raw[:].bitcast(U32).rearrange("p (m t) -> p m t", t=PACK))
+
+        qv_ps = psum.tile([P, PACK, Q], F32, name="qv_ps", tag="qv_then_a")
+        for t in range(PACK):
+            nc.tensor.matmul_mx(out=qv_ps[:, t, :], lhsT=wq_dealt[:, t, :].bitcast(FP8X4), lhsT_scale=wq_plane[:, t, :],
+                                rhs=states_codes[:].bitcast(FP8X4), rhs_scale=states_plane[:], start=True, stop=True)
+        qv_bf = pool.tile([P, Q, PACK], BF16, name="qv_bf", align_bytes=64)
+        nc.scalar.activation(qv_bf[:], qv_ps[:].rearrange("p t q -> p q t"), COPY)
+        qv_codes = pool.tile([P, Q], U32, name="qv_codes", align_bytes=64)
+        qv_plane = pool.tile([P, Q], U8, name="qv_plane", align_bytes=64)
+        nc.vector.quantize_mx(out=qv_codes[:].bitcast(FP8X4), scales=qv_plane[:],
+                              in_=qv_bf[:].rearrange("p q t -> p (q t)"))
+
+        a_sb = pool.tile([P, T], F32, name="a_sb")
+        for j in range(T // A_PIECE):
+            cols = slice(j * A_PIECE, (j + 1) * A_PIECE)
+            a_ps = psum.tile([P, A_PIECE], F32, name="a_ps", tag="qv_then_a" if j == 2 else "a%d" % j)
+            nc.tensor.matmul_mx(out=a_ps[:], lhsT=qv_codes[:].bitcast(FP8X4), lhsT_scale=qv_plane[:],
+                                rhs=cache_sb[:, 2 * cols.start : 2 * cols.stop].bitcast(FP4X4),
+                                rhs_scale=cache_plane[:, cols], start=True, stop=True)
+            if j % 2 == 0:
+                nc.vector.tensor_copy(a_sb[:, cols], a_ps[:])
+            else:
+                nc.scalar.activation(a_sb[:, cols], a_ps[:], COPY)
+
+        w = pool.tile([P, I], F32, name="w")
+        nc.scalar.activation(w[:], a_sb[:].indirect(list1[:]), COPY, scale=sa_sb[:])
+        nc.scalar.activation(f1[:].indirect(list2[:]), w[:], COPY)
+
+        bb = pool.tile([P, U], F32, name="bb")
+        for h in range(U // BANK):
+            cols = slice(h * BANK, (h + 1) * BANK)
+            b_ps = psum.tile([P, BANK], F32, name="b_ps", tag="b%d" % h)
+            nc.tensor.matmul_mx(out=b_ps[:], lhsT=qv_codes[:].bitcast(FP8X4), lhsT_scale=qv_plane[:],
+                                rhs=draft_sb[:, 4 * cols.start : 4 * cols.stop].bitcast(FP8X4),
+                                rhs_scale=draft_plane[:, cols], start=True, stop=True)
+            nc.vector.tensor_tensor(bb[:, cols], b_ps[:], f1[:, cols], ALU.subtract)
+
+        v = pool.tile([P, I], F32, name="v")
+        nc.scalar.activation(v[:], bb[:].indirect(list3[:]), COPY, scale=sb_sb[:])
+        nc.scalar.activation(f2[:].indirect(list4[:]), v[:], COPY)
+
+        cc = pool.tile([P, X], F32, name="cc")
+        for h in range(X // BANK):
+            cols = slice(h * BANK, (h + 1) * BANK)
+            c_ps = psum.tile([P, BANK], F32, name="c_ps", tag="c%d" % h)
+            nc.tensor.matmul_mx(out=c_ps[:], lhsT=states_codes[:].bitcast(FP8X4), lhsT_scale=states_plane[:],
+                                rhs=arch_sb[:, 2 * cols.start : 2 * cols.stop].bitcast(FP4X4),
+                                rhs_scale=arch_plane[:, cols], start=True, stop=True)
+            nc.vector.tensor_tensor(cc[:, cols], c_ps[:], f2[:, cols], ALU.max)
+
+        half = I // 2
+        y0 = pool.tile([P, half], F32, name="y0")
+        nc.vector.tensor_copy(y0[:], cc[:].indirect(list5[:, 0 : half // 16]))
+        nc.sync.dma_start(out[:, 0:half], y0[:])
+        y1 = pool.tile([P, half], F32, name="y1")
+        nc.scalar.activation(y1[:], cc[:].indirect(list5[:, half // 16 : I // 16]), COPY)
+        nc.scalar.dma_start(out[:, half:I], y1[:])

@@ -35,12 +35,12 @@ def tile_attend_scaledhops_sidethree_kernel(tc, states, wq_words, wq_scales, cac
             nc.vector.memset(t[:].bitcast(I32), 0)
             return t
 
-        def load_plane(plane, scales):
+        def load_plane(plane, scales, queues=(nc.sync, nc.sync, nc.sync, nc.sync)):
             for g in range(4):
-                nc.sync.dma_start(plane[32 * g : 32 * g + 4, :].bitcast(I32), scales[0, 4 * g : 4 * g + 4, :].bitcast(I32))
+                queues[g].dma_start(plane[32 * g : 32 * g + 4, :].bitcast(I32), scales[0, 4 * g : 4 * g + 4, :].bitcast(I32))
 
         def load_bytes(name, src):
-            t = pool.tile([P, src.shape[1]], U8, name=name, align_bytes=64)
+            t = pool.tile([P, src.shape[1]], U8, name=name, tag=name, align_bytes=64)
             nc.sync.dma_start(t[:].bitcast(I32), src.bitcast(I32))
             return t
 
@@ -53,14 +53,10 @@ def tile_attend_scaledhops_sidethree_kernel(tc, states, wq_words, wq_scales, cac
         cache_plane = zeroed("cache_plane", T, U8)
         draft_plane = zeroed("draft_plane", U, U8)
         arch_plane = zeroed("arch_plane", X, U8)
-        f1 = pool.tile([P, U], F32, name="f1")
-        nc.vector.memset(f1[:], 0.0)
-        f2 = pool.tile([P, X], F32, name="f2")
-        nc.vector.memset(f2[:], 0.0)
 
         states_raw = pool.tile([P, PACK, Q], F32, name="states_raw")
         nc.sync.dma_start(states_raw[:], states.rearrange("(p j) q -> p j q", j=PACK))
-        load_plane(wq_plane_raw, wq_scales)
+        load_plane(wq_plane_raw, wq_scales, (nc.sync, nc.sync, nc.scalar, nc.scalar))
         wq_raw = load_bytes("wq_raw", wq_words[0].rearrange("p n t -> p (n t)"))
         cache_sb = load_bytes("cache_sb", cache_words[0])
         load_plane(cache_plane, cache_scales)
@@ -76,36 +72,42 @@ def tile_attend_scaledhops_sidethree_kernel(tc, states, wq_words, wq_scales, cac
         load_plane(arch_plane, arch_scales)
         list5 = load_as_is("list5", offs5, U16)
 
-        wq_plane = pool.tile([P, PACK, P], U8, name="wq_plane", align_bytes=64)
-        nc.vector.tensor_copy(wq_plane[:].rearrange("p t m -> p m t"), wq_plane_raw[:].rearrange("p (m t) -> p m t", t=PACK))
-
         states_bf = pool.tile([P, Q, PACK], BF16, name="states_bf", align_bytes=64)
         nc.vector.tensor_copy(states_bf[:].rearrange("p (c i) t -> p c t i", i=4),
                               states_raw[:].rearrange("p t (c i) -> p c t i", i=4))
+        wq_plane = pool.tile([P, PACK, P], U8, name="wq_plane", align_bytes=64)
+        nc.vector.tensor_copy(wq_plane[:], wq_plane_raw[:].rearrange("p (m t) -> p t m", t=PACK))
         states_codes = pool.tile([P, Q], U32, name="states_codes", align_bytes=64)
         states_plane = pool.tile([P, Q], U8, name="states_plane", align_bytes=64)
         nc.vector.quantize_mx(out=states_codes[:].bitcast(FP8X4), scales=states_plane[:],
                               in_=states_bf[:].rearrange("p q t -> p (q t)"))
 
         wq_dealt = pool.tile([P, PACK, P], U32, name="wq_dealt", align_bytes=64)
-        nc.scalar.copy(wq_dealt[:].rearrange("p t m -> p m t"),
-                       wq_raw[:].bitcast(U32).rearrange("p (m t) -> p m t", t=PACK))
+        nc.scalar.copy(wq_dealt[:, 0:2, :].rearrange("p t (c i) -> p c t i", i=4),
+                       wq_raw[:].bitcast(U32).rearrange("p (c i t) -> p c t i", i=4, t=PACK)[:, :, 0:2, :])
+        nc.vector.tensor_copy(wq_dealt[:, 2:4, :].bitcast(I32).rearrange("p t (c i) -> p c t i", i=4),
+                              wq_raw[:].bitcast(I32).rearrange("p (c i t) -> p c t i", i=4, t=PACK)[:, :, 2:4, :])
 
-        qv_ps = psum.tile([P, PACK, Q], F32, name="qv_ps", tag="qv_then_a")
-        for t in range(PACK):
-            nc.tensor.matmul_mx(out=qv_ps[:, t, :], lhsT=wq_dealt[:, t, :].bitcast(FP8X4), lhsT_scale=wq_plane[:, t, :],
-                                rhs=states_codes[:].bitcast(FP8X4), rhs_scale=states_plane[:], start=True, stop=True)
-        qv_bf = pool.tile([P, Q, PACK], BF16, name="qv_bf", align_bytes=64)
-        nc.scalar.activation(qv_bf[:], qv_ps[:].rearrange("p t q -> p q t"), COPY)
+        qv_bf = pool.tile([P, Q, PACK], BF16, name="qv_bf", tag="qv_bf", align_bytes=64)
+        for pair in range(2):
+            qv_ps = psum.tile([P, 2, Q], F32, name="qv_ps", tag="qv_then_a%d" % pair)
+            for e in range(2):
+                t = 2 * pair + e
+                nc.tensor.matmul_mx(out=qv_ps[:, e, :], lhsT=wq_dealt[:, t, :].bitcast(FP8X4), lhsT_scale=wq_plane[:, t, :],
+                                    rhs=states_codes[:].bitcast(FP8X4), rhs_scale=states_plane[:], start=True, stop=True)
+            if pair == 0:
+                nc.vector.tensor_copy(qv_bf[:, :, 0:2], qv_ps[:].rearrange("p e q -> p q e"))
+            else:
+                nc.scalar.activation(qv_bf[:, :, 2:4], qv_ps[:].rearrange("p e q -> p q e"), COPY)
         qv_codes = pool.tile([P, Q], U32, name="qv_codes", align_bytes=64)
         qv_plane = pool.tile([P, Q], U8, name="qv_plane", align_bytes=64)
         nc.vector.quantize_mx(out=qv_codes[:].bitcast(FP8X4), scales=qv_plane[:],
                               in_=qv_bf[:].rearrange("p q t -> p (q t)"))
 
-        a_sb = pool.tile([P, T], F32, name="a_sb")
+        a_sb = pool.tile([P, T], F32, name="a_sb", tag="a_then_f2")
         for j in range(T // A_PIECE):
             cols = slice(j * A_PIECE, (j + 1) * A_PIECE)
-            a_ps = psum.tile([P, A_PIECE], F32, name="a_ps", tag="qv_then_a" if j == 2 else "a%d" % j)
+            a_ps = psum.tile([P, A_PIECE], F32, name="a_ps", tag="a%d" % j if j < 2 else "qv_then_a%d" % (j - 2))
             nc.tensor.matmul_mx(out=a_ps[:], lhsT=qv_codes[:].bitcast(FP8X4), lhsT_scale=qv_plane[:],
                                 rhs=cache_sb[:, 2 * cols.start : 2 * cols.stop].bitcast(FP4X4),
                                 rhs_scale=cache_plane[:, cols], start=True, stop=True)
@@ -114,19 +116,32 @@ def tile_attend_scaledhops_sidethree_kernel(tc, states, wq_words, wq_scales, cac
             else:
                 nc.scalar.activation(a_sb[:, cols], a_ps[:], COPY)
 
-        w = pool.tile([P, I], F32, name="w")
-        nc.scalar.activation(w[:], a_sb[:].indirect(list1[:]), COPY, scale=sa_sb[:])
-        nc.scalar.activation(f1[:].indirect(list2[:]), w[:], COPY)
+        half = I // 2
+        w = [pool.tile([P, half], F32, name="w%d" % e) for e in range(2)]
+        for e in range(2):
+            nc.scalar.activation(w[e][:], a_sb[:].indirect(list1[:, 16 * e : 16 * (e + 1)]), COPY, scale=sa_sb[:])
+        b_ps = [psum.tile([P, BANK], F32, name="b_ps%d" % h) for h in range(U // BANK)]
+        for h in range(U // BANK):
+            cols = slice(h * BANK, (h + 1) * BANK)
+            nc.tensor.matmul_mx(out=b_ps[h][:], lhsT=qv_codes[:].bitcast(FP8X4), lhsT_scale=qv_plane[:],
+                                rhs=draft_sb[:, 4 * cols.start : 4 * cols.stop].bitcast(FP8X4),
+                                rhs_scale=draft_plane[:, cols], start=True, stop=True)
+        f1 = [pool.tile([P, U], F32, name="f1_0", tag="qv_bf", align_bytes=64),
+              pool.tile([P, U], F32, name="f1_1", tag="cache_sb", align_bytes=64)]
+        for e in range(2):
+            nc.gpsimd.memset(f1[e][:], 0.0)
+        for e in range(2):
+            nc.scalar.activation(f1[e][:].indirect(list2[:, 16 * e : 16 * (e + 1)]), w[e][:], COPY)
+        b_part = pool.tile([P, U], F32, name="b_part")
 
         bb = pool.tile([P, U], F32, name="bb")
         for h in range(U // BANK):
             cols = slice(h * BANK, (h + 1) * BANK)
-            b_ps = psum.tile([P, BANK], F32, name="b_ps", tag="b%d" % h)
-            nc.tensor.matmul_mx(out=b_ps[:], lhsT=qv_codes[:].bitcast(FP8X4), lhsT_scale=qv_plane[:],
-                                rhs=draft_sb[:, 4 * cols.start : 4 * cols.stop].bitcast(FP8X4),
-                                rhs_scale=draft_plane[:, cols], start=True, stop=True)
-            nc.vector.tensor_tensor(bb[:, cols], b_ps[:], f1[:, cols], ALU.subtract)
+            nc.vector.tensor_tensor(b_part[:, cols], b_ps[h][:], f1[0][:, cols], ALU.subtract)
+        nc.vector.tensor_tensor(bb[:], b_part[:], f1[1][:], ALU.subtract)
 
+        f2 = pool.tile([P, X], F32, name="f2", tag="a_then_f2")
+        nc.gpsimd.memset(f2[:], 0.0)
         v = pool.tile([P, I], F32, name="v")
         nc.scalar.activation(v[:], bb[:].indirect(list3[:]), COPY, scale=sb_sb[:])
         nc.scalar.activation(f2[:].indirect(list4[:]), v[:], COPY)
@@ -140,7 +155,6 @@ def tile_attend_scaledhops_sidethree_kernel(tc, states, wq_words, wq_scales, cac
                                 rhs_scale=arch_plane[:, cols], start=True, stop=True)
             nc.vector.tensor_tensor(cc[:, cols], c_ps[:], f2[:, cols], ALU.max)
 
-        half = I // 2
         y0 = pool.tile([P, half], F32, name="y0")
         nc.vector.tensor_copy(y0[:], cc[:].indirect(list5[:, 0 : half // 16]))
         nc.sync.dma_start(out[:, 0:half], y0[:])

from contextlib import ExitStack

import concourse.mybir as mybir

D, K, T, U, X, I, Q = 512, 512, 1024, 1024, 1024, 512, 128
FLOPS = 2 * Q * (D * K + K * T + K * U + D * X)

F32 = mybir.dt.float32
BF16 = mybir.dt.bfloat16
I32 = mybir.dt.int32
U32 = mybir.dt.uint32
U16 = mybir.dt.uint16
U8 = mybir.dt.uint8
FP8X4 = mybir.dt.float8_e4m3fn_x4
FP4X4 = mybir.dt.float4_e2m1fn_x4
COPY = mybir.ActivationFunctionType.Copy
ALU = mybir.AluOpType

P = 128
PACK = 4
BANK = 512
A_PIECE = 256


def tile_attend_scaledhops_sidethree_kernel(tc, states, wq_words, wq_scales, cache_words, cache_scales, draft_words,
                                             draft_scales, arch_words, arch_scales, sa, sb, offs, offs2, offs3,
                                             offs4, offs5, out):
    nc = tc.nc
    with ExitStack() as ctx:
        pool = ctx.enter_context(tc.tile_pool(name="held", bufs=1))
        psum = ctx.enter_context(tc.psum_pool(name="psum", bufs=1))

        def zeroed(name, width, dtype):
            t = pool.tile([P, width], dtype, name=name, align_bytes=64)
            nc.vector.memset(t[:].bitcast(I32), 0)
            return t

        def load_plane(plane, scales, queues=(nc.sync, nc.sync, nc.sync, nc.sync)):
            for g in range(4):
                queues[g].dma_start(plane[32 * g : 32 * g + 4, :].bitcast(I32), scales[0, 4 * g : 4 * g + 4, :].bitcast(I32))

        def load_bytes(name, src):
            t = pool.tile([P, src.shape[1]], U8, name=name, tag=name, align_bytes=64)
            nc.sync.dma_start(t[:].bitcast(I32), src.bitcast(I32))
            return t

        def load_as_is(name, src, dtype):
            t = pool.tile(list(src.shape), dtype, name=name)
            nc.sync.dma_start(t[:], src)
            return t

        wq_plane_raw = zeroed("wq_plane_raw", K, U8)
        cache_plane = zeroed("cache_plane", T, U8)
        draft_plane = zeroed("draft_plane", U, U8)
        arch_plane = zeroed("arch_plane", X, U8)

        states_raw = pool.tile([P, PACK, Q], F32, name="states_raw")
        nc.sync.dma_start(states_raw[:], states.rearrange("(p j) q -> p j q", j=PACK))
        load_plane(wq_plane_raw, wq_scales, (nc.sync, nc.sync, nc.scalar, nc.scalar))
        wq_raw = load_bytes("wq_raw", wq_words[0].rearrange("p n t -> p (n t)"))
        cache_sb = load_bytes("cache_sb", cache_words[0])
        load_plane(cache_plane, cache_scales)
        list1 = load_as_is("list1", offs, U16)
        sa_sb = load_as_is("sa_sb", sa, F32)
        list2 = load_as_is("list2", offs2, U16)
        draft_sb = load_bytes("draft_sb", draft_words[0].rearrange("p n t -> p (n t)"))
        load_plane(draft_plane, draft_scales)
        list3 = load_as_is("list3", offs3, U16)
        sb_sb = load_as_is("sb_sb", sb, F32)
        list4 = load_as_is("list4", offs4, U16)
        arch_sb = load_bytes("arch_sb", arch_words[0])
        load_plane(arch_plane, arch_scales)
        list5 = load_as_is("list5", offs5, U16)

        states_bf = pool.tile([P, Q, PACK], BF16, name="states_bf", align_bytes=64)
        nc.vector.tensor_copy(states_bf[:].rearrange("p (c i) t -> p c t i", i=4),
                              states_raw[:].rearrange("p t (c i) -> p c t i", i=4))
        wq_plane = pool.tile([P, PACK, P], U8, name="wq_plane", align_bytes=64)
        nc.vector.tensor_copy(wq_plane[:], wq_plane_raw[:].rearrange("p (m t) -> p t m", t=PACK))
        states_codes = pool.tile([P, Q], U32, name="states_codes", align_bytes=64)
        states_plane = pool.tile([P, Q], U8, name="states_plane", align_bytes=64)
        nc.vector.quantize_mx(out=states_codes[:].bitcast(FP8X4), scales=states_plane[:],
                              in_=states_bf[:].rearrange("p q t -> p (q t)"))

        wq_dealt = pool.tile([P, PACK, P], U32, name="wq_dealt", align_bytes=64)
        nc.scalar.copy(wq_dealt[:, 0:2, :].rearrange("p t (c i) -> p c t i", i=4),
                       wq_raw[:].bitcast(U32).rearrange("p (c i t) -> p c t i", i=4, t=PACK)[:, :, 0:2, :])
        nc.vector.tensor_copy(wq_dealt[:, 2:4, :].bitcast(I32).rearrange("p t (c i) -> p c t i", i=4),
                              wq_raw[:].bitcast(I32).rearrange("p (c i t) -> p c t i", i=4, t=PACK)[:, :, 2:4, :])

        qv_bf = pool.tile([P, Q, PACK], BF16, name="qv_bf", tag="qv_bf", align_bytes=64)
        for pair in range(2):
            qv_ps = psum.tile([P, 2, Q], F32, name="qv_ps", tag="qv_then_a%d" % pair)
            for e in range(2):
                t = 2 * pair + e
                nc.tensor.matmul_mx(out=qv_ps[:, e, :], lhsT=wq_dealt[:, t, :].bitcast(FP8X4), lhsT_scale=wq_plane[:, t, :],
                                    rhs=states_codes[:].bitcast(FP8X4), rhs_scale=states_plane[:], start=True, stop=True)
            if pair == 0:
                nc.vector.tensor_copy(qv_bf[:, :, 0:2], qv_ps[:].rearrange("p e q -> p q e"))
            else:
                nc.scalar.activation(qv_bf[:, :, 2:4], qv_ps[:].rearrange("p e q -> p q e"), COPY)
        qv_codes = pool.tile([P, Q], U32, name="qv_codes", align_bytes=64)
        qv_plane = pool.tile([P, Q], U8, name="qv_plane", align_bytes=64)
        nc.vector.quantize_mx(out=qv_codes[:].bitcast(FP8X4), scales=qv_plane[:],
                              in_=qv_bf[:].rearrange("p q t -> p (q t)"))

        a_sb = pool.tile([P, T], F32, name="a_sb", tag="a_then_f2")
        for j in range(T // A_PIECE):
            cols = slice(j * A_PIECE, (j + 1) * A_PIECE)
            a_ps = psum.tile([P, A_PIECE], F32, name="a_ps", tag="a%d" % j if j < 2 else "qv_then_a%d" % (j - 2))
            nc.tensor.matmul_mx(out=a_ps[:], lhsT=qv_codes[:].bitcast(FP8X4), lhsT_scale=qv_plane[:],
                                rhs=cache_sb[:, 2 * cols.start : 2 * cols.stop].bitcast(FP4X4),
                                rhs_scale=cache_plane[:, cols], start=True, stop=True)
            if j % 2 == 0:
                nc.vector.tensor_copy(a_sb[:, cols], a_ps[:])
            else:
                nc.scalar.activation(a_sb[:, cols], a_ps[:], COPY)

        half = I // 2
        w = [pool.tile([P, half], F32, name="w%d" % e) for e in range(2)]
        for e in range(2):
            nc.scalar.activation(w[e][:], a_sb[:].indirect(list1[:, 16 * e : 16 * (e + 1)]), COPY, scale=sa_sb[:])
        b_ps = [psum.tile([P, BANK], F32, name="b_ps%d" % h) for h in range(U // BANK)]
        for h in range(U // BANK):
            cols = slice(h * BANK, (h + 1) * BANK)
            nc.tensor.matmul_mx(out=b_ps[h][:], lhsT=qv_codes[:].bitcast(FP8X4), lhsT_scale=qv_plane[:],
                                rhs=draft_sb[:, 4 * cols.start : 4 * cols.stop].bitcast(FP8X4),
                                rhs_scale=draft_plane[:, cols], start=True, stop=True)
        f1 = [pool.tile([P, U], F32, name="f1_0", tag="qv_bf", align_bytes=64),
              pool.tile([P, U], F32, name="f1_1", tag="cache_sb", align_bytes=64)]
        for e in range(2):
            nc.gpsimd.memset(f1[e][:], 0.0)
        for e in range(2):
            nc.scalar.activation(f1[e][:].indirect(list2[:, 16 * e : 16 * (e + 1)]), w[e][:], COPY)
        b_part = pool.tile([P, U], F32, name="b_part")

        bb = pool.tile([P, U], F32, name="bb")
        for h in range(U // BANK):
            cols = slice(h * BANK, (h + 1) * BANK)
            nc.vector.tensor_tensor(b_part[:, cols], b_ps[h][:], f1[0][:, cols], ALU.subtract)
        nc.vector.tensor_tensor(bb[:], b_part[:], f1[1][:], ALU.subtract)

        f2 = pool.tile([P, X], F32, name="f2", tag="a_then_f2")
        nc.gpsimd.memset(f2[:], 0.0)
        v = pool.tile([P, I], F32, name="v")
        nc.scalar.activation(v[:], bb[:].indirect(list3[:]), COPY, scale=sb_sb[:])
        nc.scalar.activation(f2[:].indirect(list4[:]), v[:], COPY)

        cc = pool.tile([P, X], F32, name="cc")
        for h in range(X // BANK):
            cols = slice(h * BANK, (h + 1) * BANK)
            c_ps = psum.tile([P, BANK], F32, name="c_ps", tag="c%d" % h)
            nc.tensor.matmul_mx(out=c_ps[:], lhsT=states_codes[:].bitcast(FP8X4), lhsT_scale=states_plane[:],
                                rhs=arch_sb[:, 2 * cols.start : 2 * cols.stop].bitcast(FP4X4),
                                rhs_scale=arch_plane[:, cols], start=True, stop=True)
            nc.vector.tensor_tensor(cc[:, cols], c_ps[:], f2[:, cols], ALU.max)

        y0 = pool.tile([P, half], F32, name="y0")
        nc.vector.tensor_copy(y0[:], cc[:].indirect(list5[:, 0 : half // 16]))
        nc.sync.dma_start(out[:, 0:half], y0[:])
        y1 = pool.tile([P, half], F32, name="y1")
        nc.scalar.activation(y1[:], cc[:].indirect(list5[:, half // 16 : I // 16]), COPY)
        nc.scalar.dma_start(out[:, half:I], y1[:])
